import numpy as np
import ml_dtypes


def mxq(x, axis, fmt="e4m3"):
    dtype, down = {"e4m3": (ml_dtypes.float8_e4m3fn, 7), "e5m2": (ml_dtypes.float8_e5m2, 14)}[fmt]
    v = np.moveaxis(np.asarray(x, np.float32).astype(ml_dtypes.bfloat16).astype(np.float64), axis, -1)
    blocks = v.reshape(v.shape[:-1] + (-1, 32))
    amax = np.abs(blocks).max(-1, keepdims=True)
    byte = np.maximum(np.where(amax > 0, np.frexp(amax)[1] - 1 + 127, 0) - down, 1)
    scale = np.exp2(byte - 127.0)
    codes = (blocks / scale).astype(np.float32).astype(dtype).astype(np.float64)
    return np.moveaxis((codes * scale).reshape(v.shape), -1, axis)


WIDE = False


def mx_kscale(k):
    if not WIDE:
        return np.ones(k)
    levels = np.array([10, -10, 5, -5, 0])
    if k % 512:
        return np.exp2(np.random.permutation(np.resize(levels, k // 32))).repeat(32)
    a = np.empty((k // 512, 16))
    for p in range(k // 512):
        a[p, :8] = np.random.permutation(np.resize(levels, 8))
        for g in range(8):
            far = levels[np.abs(levels - a[p, g]) >= 10]
            a[p, g + 8] = far[np.random.randint(len(far))]
    return np.exp2(a.ravel()).repeat(32)


def f64(x):
    return np.asarray(x).astype(np.float64)


def striped(idx):
    return np.tile(idx.reshape(-1, 16).T, (8, 1)).astype(np.uint16)


def unstriped(offs):
    return offs[:16].T.reshape(-1).astype(np.int64)


def pack_weight(w):
    k, n = w.shape
    w = f64(np.asarray(w, np.float32).astype(ml_dtypes.bfloat16)).reshape(k // 32, 32, n)
    amax = np.abs(w).max(1)
    byte = np.clip(np.where(amax > 0, np.frexp(amax)[1] - 1 + 127 - 7, 1), 1, 254)
    scaled = (w * np.exp2(127.0 - byte)[:, None, :]).reshape(k, n).astype(np.float32)
    words = np.ascontiguousarray(scaled.reshape(k // 512, 128, 4, n).transpose(0, 1, 3, 2)).astype(ml_dtypes.float8_e4m3fn).view(np.uint8)
    return words, np.ascontiguousarray(byte.astype(np.uint8).reshape(k // 512, 16, n))


def unpack_weight(words, scales):
    g, p, n, _ = words.shape
    vals = np.ascontiguousarray(words).view(ml_dtypes.float8_e4m3fn).astype(np.float64) * np.repeat(np.exp2(scales.astype(np.float64) - 127.0), 8, axis=1)[..., None]
    return vals.transpose(0, 1, 3, 2).reshape(g * 512, n)


K, T, S, H, W, C = 512, 2048, 512, 512, 256, 512


def setup_inputs():
    n = np.random.standard_normal
    s = mx_kscale(K)[:, None]
    packed_xT = pack_weight(n((K, T)) * s)
    return {
        "x_words": packed_xT[0],
        "x_scales": packed_xT[1],
        "w1": (n((K, H)) / np.sqrt(K) / s).astype(np.float32),
        "w2": (n((K, H)) / np.sqrt(K) / s).astype(np.float32),
        "gs": (np.random.uniform(0.5, 1.5, (K, 1)) / s).astype(np.float32),
        "offs": striped(np.random.permutation(T)[:S]),
        "two": striped(np.random.permutation(T)[:S]),
        "n1": striped(np.random.permutation(S)[:W]),
        "n2": striped(np.random.permutation(S)[:W]),
        "cand": striped(np.random.permutation(T)[:C]),
        "n3": striped(np.random.permutation(S)),
        "n4": striped(np.random.permutation(S)),
    }


def reference(x_words, x_scales, w1, w2, gs, offs, two, n1, n2, cand, n3, n4):
    x_cand = unpack_weight(x_words, x_scales)[:, unstriped(cand)]
    x_two = unpack_weight(x_words, x_scales)[:, unstriped(two)]
    d = mxq(f64(w2), 0, "e4m3").T @ x_two
    xq = unpack_weight(x_words, x_scales)[:, unstriped(offs)]
    y = mxq(f64(w1), 0, "e4m3").T @ xq
    ra = d[:, unstriped(n2)] - (0.5 * y[:, unstriped(n1)])
    ds = y.copy()
    ds[:, unstriped(n1)] = ra
    z = f64(gs) * ds
    s = 0.0625 * ((x_cand.T @ mxq(z, 0, "e4m3")))
    return s[:, unstriped(n3)] - s[:, unstriped(n4)]

@@ -1,0 +1,178 @@
+from contextlib import ExitStack
+
+import concourse.mybir as mybir
+
+K, T, S, H, W, C = 512, 2048, 512, 512, 256, 512
+FLOPS = 2 * K * H * S * 2 + 2 * H * C * S
+
+F32 = mybir.dt.float32
+BF16 = mybir.dt.bfloat16
+I32 = mybir.dt.int32
+U32 = mybir.dt.uint32
+U16 = mybir.dt.uint16
+U8 = mybir.dt.uint8
+FP8X4 = mybir.dt.float8_e4m3fn_x4
+COPY = mybir.ActivationFunctionType.Copy
+MULT = mybir.AluOpType.mult
+SUB = mybir.AluOpType.subtract
+ADD = mybir.AluOpType.add
+
+P = 128
+PACK = 4
+HALF = 256
+
+
+def tile_picked_twcputbgap_none_p_kernel(
+    tc, x_words, x_scales, w1, w2, gs, offs, two, n1, n2, cand, n3, n4, out
+):
+    nc = tc.nc
+    with ExitStack() as ctx:
+        keep = ctx.enter_context(tc.tile_pool(name="keep", bufs=1))
+        psum = ctx.enter_context(tc.psum_pool(name="psum", bufs=8))
+
+        def load_list(src, name):
+            tile = keep.tile(list(src.shape), U16, name=name)
+            nc.sync.dma_start(tile[:], src)
+            return tile
+
+        def load_weight_half(w, h, name):
+            raw = keep.tile([P, PACK, HALF], F32, name=name)
+            nc.sync.dma_start(raw[:], w.rearrange("(p j) c -> p j c", j=PACK)[:, :, h * HALF : (h + 1) * HALF])
+            return raw
+
+        scale_table = keep.tile([P, T], U8, name="scale_table")
+        nc.gpsimd.memset(scale_table[:].bitcast(I32), 0)
+        two_t = load_list(two, "two_t")
+        offs_t = load_list(offs, "offs_t")
+        w2_raw = [load_weight_half(w2, 0, "w2_raw0")]
+        for q in range(4):
+            nc.sync.dma_start(
+                scale_table[32 * q : 32 * q + 4, :].bitcast(I32), x_scales[0, 4 * q : 4 * q + 4, :].bitcast(I32)
+            )
+        w2_raw.append(load_weight_half(w2, 1, "w2_raw1"))
+        cand_t = load_list(cand, "cand_t")
+        word_table = keep.tile([P, T], U32, name="word_table")
+        nc.sync.dma_start(word_table[:].bitcast(I32), x_words[0].rearrange("p n t -> p (n t)").bitcast(I32))
+        w1_raw = [load_weight_half(w1, h, "w1_raw%d" % h) for h in range(2)]
+        n2_t = load_list(n2, "n2_t")
+        n1_t = load_list(n1, "n1_t")
+        gs_t = keep.tile([P, PACK], F32, name="gs_t")
+        nc.sync.dma_start(gs_t[:], gs.rearrange("(p t) o -> p (t o)", t=PACK))
+        n3_t = load_list(n3, "n3_t")
+        n4_t = load_list(n4, "n4_t")
+
+        minus_half = keep.tile([P, W], F32, name="minus_half")
+        nc.gpsimd.memset(minus_half[:], -0.5)
+
+        def pick_scales(lst, name):
+            picked = keep.tile([P, S], U8, name=name, align_bytes=64)
+            nc.vector.tensor_copy(picked[:], scale_table[:].indirect(lst[:]))
+            return picked
+
+        def pick_words(lst, name):
+            picked = keep.tile([P, S], U32, name=name, align_bytes=64)
+            nc.vector.tensor_copy(picked[:], word_table[:].indirect(lst[:]))
+            return picked
+
+        def deal_weight(grouped, raw, h, on_scalar):
+            dst = grouped[:].rearrange("p (t m j) -> p m j t", t=PACK, j=PACK)[:, h * 64 : (h + 1) * 64]
+            src = raw[:].rearrange("p j (m t) -> p m j t", t=PACK)
+            if on_scalar:
+                nc.scalar.copy(dst, src)
+            else:
+                nc.vector.tensor_copy(dst, src)
+
+        def quantise(grouped, name):
+            codes = keep.tile([P, 512], U32, name=name + "_codes", align_bytes=64)
+            scales = keep.tile([P, 512], U8, name=name + "_scales", align_bytes=64)
+            nc.vector.quantize_mx(out=codes[:].bitcast(FP8X4), scales=scales[:], in_=grouped)
+            return codes, scales
+
+        def product(lhs, lhs_scales, t, rhs, rhs_scales):
+            acc = psum.tile([P, 512], F32, name="acc")
+            cols = slice(t * P, (t + 1) * P)
+            nc.tensor.matmul_mx(
+                out=acc[:],
+                lhsT=lhs[:, cols].bitcast(FP8X4),
+                lhsT_scale=lhs_scales[:, cols],
+                rhs=rhs[:].bitcast(FP8X4),
+                rhs_scale=rhs_scales[:],
+                start=True,
+                stop=True,
+            )
+            return acc
+
+        two_scales = pick_scales(two_t, "two_scales")
+        offs_scales = pick_scales(offs_t, "offs_scales")
+        cand_scales = pick_scales(cand_t, "cand_scales")
+        w2_grouped = keep.tile([P, PACK * H], BF16, name="w2_grouped", align_bytes=64)
+        w1_grouped = keep.tile([P, PACK * H], BF16, name="w1_grouped", align_bytes=64)
+        deal_weight(w2_grouped, w2_raw[0], 0, True)
+        deal_weight(w2_grouped, w2_raw[1], 1, True)
+        w2_codes, w2_scales = quantise(w2_grouped[:], "w2")
+        two_words = pick_words(two_t, "two_words")
+        offs_words = pick_words(offs_t, "offs_words")
+        deal_weight(w1_grouped, w1_raw[0], 0, True)
+        deal_weight(w1_grouped, w1_raw[1], 1, False)
+        w1_codes, w1_scales = quantise(w1_grouped[:], "w1")
+        cand_words = pick_words(cand_t, "cand_words")
+
+        d_acc = [product(w2_codes, w2_scales, t, two_words, two_scales) for t in range(PACK)]
+        y_acc = [product(w1_codes, w1_scales, t, offs_words, offs_scales) for t in range(PACK)]
+
+        pairs = keep.tile([P, 2, S, 2], BF16, name="pairs")
+
+        def fetch_d(t, factor):
+            d_rows = keep.tile([P, S], F32, name="d_rows%d" % t)
+            nc.scalar.copy(d_rows[:], d_acc[t][:])
+            d_picked = keep.tile([P, W], F32, name="d_picked%d" % t)
+            nc.scalar.activation(d_picked[:], d_rows[:].indirect(n2_t[:]), COPY, scale=factor)
+            return d_picked
+
+        def weigh(t, ds):
+            nc.vector.tensor_scalar(pairs[:, t // 2, :, t % 2], ds[:], gs_t[:, t : t + 1], None, MULT)
+
+        ds = [keep.tile([P, S], F32, name="ds%d" % t) for t in range(PACK)]
+        gaps = []
+        for t in range(2):
+            d_picked = fetch_d(t, 2.0)
+            if t == 0:
+                nc.vector.tensor_copy(ds[t][:], y_acc[t][:])
+            else:
+                nc.scalar.copy(ds[t][:], y_acc[t][:])
+            gap = keep.tile([P, W], F32, name="gap%d" % t)
+            nc.vector.tensor_tensor(gap[:], ds[t][:].indirect(n1_t[:]), d_picked[:], SUB)
+            gaps.append(gap)
+        nc.vector.tensor_tensor(ds[0][:].indirect(n1_t[:]), gaps[0][:], minus_half[:], MULT)
+        weigh(0, ds[0])
+        for t in range(2, PACK):
+            d_picked = fetch_d(t, 1.0)
+            nc.scalar.copy(ds[t][:], y_acc[t][:])
+            y_picked = keep.tile([P, W], F32, name="y_picked%d" % t)
+            nc.scalar.activation(y_picked[:], ds[t][:].indirect(n1_t[:]), COPY, scale=-0.5)
+            nc.vector.tensor_tensor(ds[t][:].indirect(n1_t[:]), d_picked[:], y_picked[:], ADD)
+            weigh(t, ds[t])
+        nc.scalar.activation(ds[1][:].indirect(n1_t[:]), gaps[1][:], COPY, scale=-0.5)
+        weigh(1, ds[1])
+
+        z_grouped = keep.tile([P, PACK * S], BF16, name="z_grouped", align_bytes=64)
+        nc.vector.tensor_copy(
+            z_grouped[:].bitcast(F32).rearrange("p (j u) -> p j u", u=2),
+            pairs[:].rearrange("p u j e -> p (u j e)").bitcast(F32).rearrange("p (u j) -> p j u", u=2),
+        )
+        z_codes, z_scales = quantise(z_grouped[:], "z")
+
+        for c in range(C // P):
+            s_acc = product(cand_words, cand_scales, c, z_codes, z_scales)
+            minus_s = keep.tile([P, S], F32, name="minus_s%d" % c)
+            if c in (1, 2):
+                nc.vector.tensor_scalar(minus_s[:], s_acc[:], -0.0625, None, MULT)
+            else:
+                nc.scalar.activation(minus_s[:], s_acc[:], COPY, scale=-0.0625)
+            for h in range(2):
+                lcols = slice(h * 16, (h + 1) * 16)
+                first = keep.tile([P, HALF], F32, name="first%d_%d" % (c, h))
+                nc.scalar.activation(first[:], minus_s[:].indirect(n3_t[:, lcols]), COPY)
+                result = keep.tile([P, HALF], F32, name="result%d_%d" % (c, h))
+                nc.vector.tensor_tensor(result[:], minus_s[:].indirect(n4_t[:, lcols]), first[:], SUB)
+                nc.sync.dma_start(out[c * P : (c + 1) * P, h * HALF : (h + 1) * HALF], result[:])

@@ -28,32 +28,35 @@ def tile_picked_twcputbgap_none_p_kernel(
     nc = tc.nc
     with ExitStack() as ctx:
         keep = ctx.enter_context(tc.tile_pool(name="keep", bufs=1))
-        psum = ctx.enter_context(tc.psum_pool(name="psum", bufs=8))
+        psum = ctx.enter_context(tc.psum_pool(name="psum", bufs=1))
+        reuse = ctx.enter_context(tc.tile_pool(name="reuse", bufs=1))
 
         def load_list(src, name):
             tile = keep.tile(list(src.shape), U16, name=name)
             nc.sync.dma_start(tile[:], src)
             return tile
 
-        def load_weight_half(w, h, name):
-            raw = keep.tile([P, PACK, HALF], F32, name=name)
+        def load_weight_half(w, h, name, raw=None):
+            if raw is None:
+                raw = keep.tile([P, PACK, HALF], F32, name=name)
             nc.sync.dma_start(raw[:], w.rearrange("(p j) c -> p j c", j=PACK)[:, :, h * HALF : (h + 1) * HALF])
             return raw
 
         scale_table = keep.tile([P, T], U8, name="scale_table")
         nc.gpsimd.memset(scale_table[:].bitcast(I32), 0)
         two_t = load_list(two, "two_t")
-        offs_t = load_list(offs, "offs_t")
         w2_raw = [load_weight_half(w2, 0, "w2_raw0")]
         for q in range(4):
             nc.sync.dma_start(
                 scale_table[32 * q : 32 * q + 4, :].bitcast(I32), x_scales[0, 4 * q : 4 * q + 4, :].bitcast(I32)
             )
+        offs_t = load_list(offs, "offs_t")
         w2_raw.append(load_weight_half(w2, 1, "w2_raw1"))
-        cand_t = load_list(cand, "cand_t")
         word_table = keep.tile([P, T], U32, name="word_table")
         nc.sync.dma_start(word_table[:].bitcast(I32), x_words[0].rearrange("p n t -> p (n t)").bitcast(I32))
-        w1_raw = [load_weight_half(w1, h, "w1_raw%d" % h) for h in range(2)]
+        w1_raw = [load_weight_half(w1, 0, "w1_raw0", reuse.tile([P, PACK, HALF], F32, name="w1_raw0", offset=4096))]
+        w1_raw.append(load_weight_half(w1, 1, "w1_raw1"))
+        cand_t = load_list(cand, "cand_t")
         n2_t = load_list(n2, "n2_t")
         n1_t = load_list(n1, "n1_t")
         gs_t = keep.tile([P, PACK], F32, name="gs_t")
@@ -61,18 +64,19 @@ def tile_picked_twcputbgap_none_p_kernel(
         n3_t = load_list(n3, "n3_t")
         n4_t = load_list(n4, "n4_t")
 
+
         minus_half = keep.tile([P, W], F32, name="minus_half")
         nc.gpsimd.memset(minus_half[:], -0.5)
 
-        def pick_scales(lst, name):
-            picked = keep.tile([P, S], U8, name=name, align_bytes=64)
-            nc.vector.tensor_copy(picked[:], scale_table[:].indirect(lst[:]))
+        def pick(table, lst, picked):
+            nc.vector.tensor_copy(picked[:], table[:].indirect(lst))
             return picked
 
+        def pick_scales(lst, name):
+            return pick(scale_table, lst[:], keep.tile([P, S], U8, name=name, align_bytes=64))
+
         def pick_words(lst, name):
-            picked = keep.tile([P, S], U32, name=name, align_bytes=64)
-            nc.vector.tensor_copy(picked[:], word_table[:].indirect(lst[:]))
-            return picked
+            return pick(word_table, lst[:], keep.tile([P, S], U32, name=name, align_bytes=64))
 
         def deal_weight(grouped, raw, h, on_scalar):
             dst = grouped[:].rearrange("p (t m j) -> p m j t", t=PACK, j=PACK)[:, h * 64 : (h + 1) * 64]
@@ -88,8 +92,8 @@ def tile_picked_twcputbgap_none_p_kernel(
             nc.vector.quantize_mx(out=codes[:].bitcast(FP8X4), scales=scales[:], in_=grouped)
             return codes, scales
 
-        def product(lhs, lhs_scales, t, rhs, rhs_scales):
-            acc = psum.tile([P, 512], F32, name="acc")
+        def product(lhs, lhs_scales, t, rhs, rhs_scales, bank):
+            acc = psum.tile([P, 512], F32, name="acc", tag="bank%d" % bank)
             cols = slice(t * P, (t + 1) * P)
             nc.tensor.matmul_mx(
                 out=acc[:],
@@ -104,9 +108,8 @@ def tile_picked_twcputbgap_none_p_kernel(
 
         two_scales = pick_scales(two_t, "two_scales")
         offs_scales = pick_scales(offs_t, "offs_scales")
-        cand_scales = pick_scales(cand_t, "cand_scales")
         w2_grouped = keep.tile([P, PACK * H], BF16, name="w2_grouped", align_bytes=64)
-        w1_grouped = keep.tile([P, PACK * H], BF16, name="w1_grouped", align_bytes=64)
+        w1_grouped = reuse.tile([P, PACK * H], BF16, name="w1_grouped", align_bytes=64, offset=0)
         deal_weight(w2_grouped, w2_raw[0], 0, True)
         deal_weight(w2_grouped, w2_raw[1], 1, True)
         w2_codes, w2_scales = quantise(w2_grouped[:], "w2")
@@ -115,64 +118,107 @@ def tile_picked_twcputbgap_none_p_kernel(
         deal_weight(w1_grouped, w1_raw[0], 0, True)
         deal_weight(w1_grouped, w1_raw[1], 1, False)
         w1_codes, w1_scales = quantise(w1_grouped[:], "w1")
-        cand_words = pick_words(cand_t, "cand_words")
+        cand_words = [pick(word_table, cand_t[:, :16], reuse.tile([P, HALF], U32, name="cand_words0", align_bytes=64, offset=0))]
+        cand_scales = pick(scale_table, cand_t[:], reuse.tile([P, C], U8, name="cand_scales", align_bytes=64, offset=4 * C))
 
-        d_acc = [product(w2_codes, w2_scales, t, two_words, two_scales) for t in range(PACK)]
-        y_acc = [product(w1_codes, w1_scales, t, offs_words, offs_scales) for t in range(PACK)]
+        d_acc = [product(w2_codes, w2_scales, t, two_words, two_scales, t) for t in range(2)]
+        y_acc = [product(w1_codes, w1_scales, t, offs_words, offs_scales, 2 + t) for t in range(PACK)]
 
-        pairs = keep.tile([P, 2, S, 2], BF16, name="pairs")
+        z_planes = keep.tile([P, PACK, S], BF16, name="z_planes")
 
-        def fetch_d(t, factor):
-            d_rows = keep.tile([P, S], F32, name="d_rows%d" % t)
+        def empty_d(t):
+            if t < 2:
+                d_rows = reuse.tile([P, S], F32, name="d_rows%d" % t, offset=4096 + 2048 * t)
+            else:
+                d_rows = keep.tile([P, S], F32, name="d_rows%d" % t)
             nc.scalar.copy(d_rows[:], d_acc[t][:])
-            d_picked = keep.tile([P, W], F32, name="d_picked%d" % t)
-            nc.scalar.activation(d_picked[:], d_rows[:].indirect(n2_t[:]), COPY, scale=factor)
-            return d_picked
+            return d_rows
 
-        def weigh(t, ds):
-            nc.vector.tensor_scalar(pairs[:, t // 2, :, t % 2], ds[:], gs_t[:, t : t + 1], None, MULT)
+        def fetch(rows, lst, factor, name):
+            picked = keep.tile([P, W], F32, name=name)
+            nc.scalar.activation(picked[:], rows[:].indirect(lst[:]), COPY, scale=factor)
+            return picked
+
+        def weigh(t):
+            nc.vector.tensor_scalar(z_planes[:, t, :], ds[t][:], gs_t[:, t : t + 1], None, MULT)
+
+        def update(t, d_picked):
+            y_picked = fetch(ds[t], n1_t, -0.5, "y_picked%d" % t)
+            nc.vector.tensor_tensor(ds[t][:].indirect(n1_t[:]), d_picked[:], y_picked[:], ADD)
+            weigh(t)
 
         ds = [keep.tile([P, S], F32, name="ds%d" % t) for t in range(PACK)]
-        gaps = []
+        d_rows = [empty_d(t) for t in range(2)]
+        d_picked0 = fetch(d_rows[0], n2_t, 2.0, "d_picked0")
+        d_twice1 = fetch(d_rows[1], n2_t, 2.0, "d_twice1")
         for t in range(2):
-            d_picked = fetch_d(t, 2.0)
-            if t == 0:
-                nc.vector.tensor_copy(ds[t][:], y_acc[t][:])
-            else:
-                nc.scalar.copy(ds[t][:], y_acc[t][:])
-            gap = keep.tile([P, W], F32, name="gap%d" % t)
-            nc.vector.tensor_tensor(gap[:], ds[t][:].indirect(n1_t[:]), d_picked[:], SUB)
-            gaps.append(gap)
-        nc.vector.tensor_tensor(ds[0][:].indirect(n1_t[:]), gaps[0][:], minus_half[:], MULT)
-        weigh(0, ds[0])
-        for t in range(2, PACK):
-            d_picked = fetch_d(t, 1.0)
             nc.scalar.copy(ds[t][:], y_acc[t][:])
-            y_picked = keep.tile([P, W], F32, name="y_picked%d" % t)
-            nc.scalar.activation(y_picked[:], ds[t][:].indirect(n1_t[:]), COPY, scale=-0.5)
-            nc.vector.tensor_tensor(ds[t][:].indirect(n1_t[:]), d_picked[:], y_picked[:], ADD)
-            weigh(t, ds[t])
-        nc.scalar.activation(ds[1][:].indirect(n1_t[:]), gaps[1][:], COPY, scale=-0.5)
-        weigh(1, ds[1])
+            d_acc.append(product(w2_codes, w2_scales, 2 + t, two_words, two_scales, 2 + t))
+        gap0 = keep.tile([P, W], F32, name="gap0")
+        nc.vector.tensor_tensor(gap0[:], ds[0][:].indirect(n1_t[:]), d_picked0[:], SUB)
+        nc.vector.tensor_tensor(ds[0][:].indirect(n1_t[:]), gap0[:], minus_half[:], MULT)
+        weigh(0)
+        gap1 = keep.tile([P, W], F32, name="gap1")
+        nc.vector.tensor_tensor(gap1[:], ds[1][:].indirect(n1_t[:]), d_twice1[:], SUB)
+        for t in range(2, PACK):
+            rows = empty_d(t)
+            nc.scalar.copy(ds[t][:], y_acc[t][:])
+            update(t, fetch(rows, n2_t, 1.0, "d_picked%d" % t))
+        nc.scalar.activation(ds[1][:].indirect(n1_t[:]), gap1[:], COPY, scale=-0.5)
+        nc.scalar.activation(z_planes[:, 1, :], ds[1][:], COPY, scale=gs_t[:, 1:2])
 
-        z_grouped = keep.tile([P, PACK * S], BF16, name="z_grouped", align_bytes=64)
-        nc.vector.tensor_copy(
-            z_grouped[:].bitcast(F32).rearrange("p (j u) -> p j u", u=2),
-            pairs[:].rearrange("p u j e -> p (u j e)").bitcast(F32).rearrange("p (u j) -> p j u", u=2),
+        z_grouped = reuse.tile([P, PACK * S], BF16, name="z_grouped", align_bytes=64, offset=8192)
+        z_codes = keep.tile([P, S], U32, name="z_codes", align_bytes=64)
+        z_scales = keep.tile([P, S], U8, name="z_scales", align_bytes=64)
+        for h in range(2):
+            runs = slice(h * HALF // 4, (h + 1) * HALF // 4)
+            dst = z_grouped[:].rearrange("p (c i t) -> p c t i", i=4, t=PACK)[:, runs]
+            src = z_planes[:].rearrange("p t (c i) -> p c t i", i=4)[:, runs]
+            if h == 0:
+                nc.vector.tensor_copy(dst, src)
+            else:
+                nc.scalar.copy(dst, src)
+        for h in range(2):
+            cols = slice(h * HALF, (h + 1) * HALF)
+            nc.vector.quantize_mx(
+                out=z_codes[:, cols].bitcast(FP8X4),
+                scales=z_scales[:, cols],
+                in_=z_grouped[:, PACK * h * HALF : PACK * (h + 1) * HALF],
+            )
+
+        cand_words.append(
+            pick(word_table, cand_t[:, 16:], reuse.tile([P, HALF], U32, name="cand_words1", align_bytes=64, offset=8192 + 2048))
         )
-        z_codes, z_scales = quantise(z_grouped[:], "z")
+
+        def score(c, cols, bank):
+            width = cols.stop - cols.start
+            acc = psum.tile([P, width], F32, name="acc", tag="bank%d" % bank)
+            rows = slice(c * P, (c + 1) * P)
+            nc.tensor.matmul_mx(
+                out=acc[:],
+                lhsT=cand_words[c // 2][:, (c % 2) * P : (c % 2 + 1) * P].bitcast(FP8X4),
+                lhsT_scale=cand_scales[:, rows],
+                rhs=z_codes[:, cols].bitcast(FP8X4),
+                rhs_scale=z_scales[:, cols],
+                start=True,
+                stop=True,
+            )
+            return acc
 
         for c in range(C // P):
-            s_acc = product(cand_words, cand_scales, c, z_codes, z_scales)
             minus_s = keep.tile([P, S], F32, name="minus_s%d" % c)
-            if c in (1, 2):
-                nc.vector.tensor_scalar(minus_s[:], s_acc[:], -0.0625, None, MULT)
+            if c == 0:
+                nc.scalar.activation(minus_s[:, :HALF], score(c, slice(0, HALF), 0)[:], COPY, scale=-0.0625)
+                nc.vector.tensor_scalar(minus_s[:, HALF:], score(c, slice(HALF, S), 1)[:], -0.0625, None, MULT)
+            elif c < 3:
+                nc.vector.tensor_scalar(minus_s[:], score(c, slice(0, S), 3 + c)[:], -0.0625, None, MULT)
             else:
-                nc.scalar.activation(minus_s[:], s_acc[:], COPY, scale=-0.0625)
-            for h in range(2):
-                lcols = slice(h * 16, (h + 1) * 16)
-                first = keep.tile([P, HALF], F32, name="first%d_%d" % (c, h))
+                nc.scalar.activation(minus_s[:], score(c, slice(0, S), 3 + c)[:], COPY, scale=-0.0625)
+            edges = (0, 256, 512) if c < 3 else (0, 256, 384, 512)
+            for lo, hi in zip(edges, edges[1:]):
+                lcols = slice(lo // 16, hi // 16)
+                first = keep.tile([P, hi - lo], F32, name="first%d_%d" % (c, lo))
                 nc.scalar.activation(first[:], minus_s[:].indirect(n3_t[:, lcols]), COPY)
-                result = keep.tile([P, HALF], F32, name="result%d_%d" % (c, h))
+                result = keep.tile([P, hi - lo], F32, name="result%d_%d" % (c, lo))
                 nc.vector.tensor_tensor(result[:], minus_s[:].indirect(n4_t[:, lcols]), first[:], SUB)
-                nc.sync.dma_start(out[c * P : (c + 1) * P, h * HALF : (h + 1) * HALF], result[:])
+                nc.sync.dma_start(out[c * P : (c + 1) * P, lo:hi], result[:])

@@ -55,7 +55,7 @@ def tile_picked_twcputbgap_none_p_kernel(
         word_table = keep.tile([P, T], U32, name="word_table")
         nc.sync.dma_start(word_table[:].bitcast(I32), x_words[0].rearrange("p n t -> p (n t)").bitcast(I32))
         w1_raw = [load_weight_half(w1, 0, "w1_raw0", reuse.tile([P, PACK, HALF], F32, name="w1_raw0", offset=4096))]
-        w1_raw.append(load_weight_half(w1, 1, "w1_raw1"))
+        w1_raw.append(load_weight_half(w1, 1, "w1_raw1", reuse.tile([P, PACK, HALF], F32, name="w1_raw1", offset=0)))
         cand_t = load_list(cand, "cand_t")
         n2_t = load_list(n2, "n2_t")
         n1_t = load_list(n1, "n1_t")
@@ -67,6 +67,10 @@ def tile_picked_twcputbgap_none_p_kernel(
 
         minus_half = keep.tile([P, W], F32, name="minus_half")
         nc.gpsimd.memset(minus_half[:], -0.5)
+
+        minus_s = [keep.tile([P, S + 16], F32, name="minus_s%d" % c) for c in range(C // P)]
+        for tile in minus_s:
+            nc.gpsimd.memset(tile[:, S:], 0.0)
 
         def pick(table, lst, picked):
             nc.vector.tensor_copy(picked[:], table[:].indirect(lst))
@@ -109,7 +113,7 @@ def tile_picked_twcputbgap_none_p_kernel(
         two_scales = pick_scales(two_t, "two_scales")
         offs_scales = pick_scales(offs_t, "offs_scales")
         w2_grouped = keep.tile([P, PACK * H], BF16, name="w2_grouped", align_bytes=64)
-        w1_grouped = reuse.tile([P, PACK * H], BF16, name="w1_grouped", align_bytes=64, offset=0)
+        w1_grouped = keep.tile([P, PACK * H], BF16, name="w1_grouped", align_bytes=64)
         deal_weight(w2_grouped, w2_raw[0], 0, True)
         deal_weight(w2_grouped, w2_raw[1], 1, True)
         w2_codes, w2_scales = quantise(w2_grouped[:], "w2")
@@ -124,10 +128,9 @@ def tile_picked_twcputbgap_none_p_kernel(
         d_acc = [product(w2_codes, w2_scales, t, two_words, two_scales, t) for t in range(2)]
         y_acc = [product(w1_codes, w1_scales, t, offs_words, offs_scales, 2 + t) for t in range(PACK)]
 
-        z_planes = keep.tile([P, PACK, S], BF16, name="z_planes")
 
         def empty_d(t):
-            if t < 2:
+            if t < 3:
                 d_rows = reuse.tile([P, S], F32, name="d_rows%d" % t, offset=4096 + 2048 * t)
             else:
                 d_rows = keep.tile([P, S], F32, name="d_rows%d" % t)
@@ -139,45 +142,38 @@ def tile_picked_twcputbgap_none_p_kernel(
             nc.scalar.activation(picked[:], rows[:].indirect(lst[:]), COPY, scale=factor)
             return picked
 
-        def weigh(t):
-            nc.vector.tensor_scalar(z_planes[:, t, :], ds[t][:], gs_t[:, t : t + 1], None, MULT)
-
-        def update(t, d_picked):
-            y_picked = fetch(ds[t], n1_t, -0.5, "y_picked%d" % t)
-            nc.vector.tensor_tensor(ds[t][:].indirect(n1_t[:]), d_picked[:], y_picked[:], ADD)
-            weigh(t)
-
         ds = [keep.tile([P, S], F32, name="ds%d" % t) for t in range(PACK)]
         d_rows = [empty_d(t) for t in range(2)]
-        d_picked0 = fetch(d_rows[0], n2_t, 2.0, "d_picked0")
-        d_twice1 = fetch(d_rows[1], n2_t, 2.0, "d_twice1")
+        d_twice = [fetch(d_rows[t], n2_t, 2.0, "d_twice%d" % t) for t in range(2)]
         for t in range(2):
             nc.scalar.copy(ds[t][:], y_acc[t][:])
             d_acc.append(product(w2_codes, w2_scales, 2 + t, two_words, two_scales, 2 + t))
-        gap0 = keep.tile([P, W], F32, name="gap0")
-        nc.vector.tensor_tensor(gap0[:], ds[0][:].indirect(n1_t[:]), d_picked0[:], SUB)
-        nc.vector.tensor_tensor(ds[0][:].indirect(n1_t[:]), gap0[:], minus_half[:], MULT)
-        weigh(0)
-        gap1 = keep.tile([P, W], F32, name="gap1")
-        nc.vector.tensor_tensor(gap1[:], ds[1][:].indirect(n1_t[:]), d_twice1[:], SUB)
+        gaps = []
+        for t in range(2):
+            gap = keep.tile([P, W], F32, name="gap%d" % t)
+            nc.vector.tensor_tensor(gap[:], ds[t][:].indirect(n1_t[:]), d_twice[t][:], SUB)
+            gaps.append(gap)
+        nc.vector.tensor_tensor(ds[0][:].indirect(n1_t[:]), gaps[0][:], minus_half[:], MULT)
         for t in range(2, PACK):
-            rows = empty_d(t)
             nc.scalar.copy(ds[t][:], y_acc[t][:])
-            update(t, fetch(rows, n2_t, 1.0, "d_picked%d" % t))
-        nc.scalar.activation(ds[1][:].indirect(n1_t[:]), gap1[:], COPY, scale=-0.5)
+            rows = empty_d(t)
+            y_picked = fetch(ds[t], n1_t, -0.5, "y_picked%d" % t)
+            d_picked = fetch(rows, n2_t, 1.0, "d_picked%d" % t)
+            nc.vector.tensor_tensor(ds[t][:].indirect(n1_t[:]), d_picked[:], y_picked[:], ADD)
+        nc.scalar.activation(ds[1][:].indirect(n1_t[:]), gaps[1][:], COPY, scale=-0.5)
+        z_planes = reuse.tile([P, PACK, S], BF16, name="z_planes", offset=8192)
+        for t in (0, 2, 3):
+            nc.vector.tensor_scalar(z_planes[:, t, :], ds[t][:], gs_t[:, t : t + 1], None, MULT)
         nc.scalar.activation(z_planes[:, 1, :], ds[1][:], COPY, scale=gs_t[:, 1:2])
 
-        z_grouped = reuse.tile([P, PACK * S], BF16, name="z_grouped", align_bytes=64, offset=8192)
+        z_grouped = keep.tile([P, PACK * S], BF16, name="z_grouped", align_bytes=64)
         z_codes = keep.tile([P, S], U32, name="z_codes", align_bytes=64)
         z_scales = keep.tile([P, S], U8, name="z_scales", align_bytes=64)
-        for h in range(2):
-            runs = slice(h * HALF // 4, (h + 1) * HALF // 4)
-            dst = z_grouped[:].rearrange("p (c i t) -> p c t i", i=4, t=PACK)[:, runs]
-            src = z_planes[:].rearrange("p t (c i) -> p c t i", i=4)[:, runs]
-            if h == 0:
-                nc.vector.tensor_copy(dst, src)
-            else:
-                nc.scalar.copy(dst, src)
+        dst = z_grouped[:].rearrange("p (c i t) -> p c t i", i=4, t=PACK)
+        src = z_planes[:].rearrange("p t (c i) -> p c t i", i=4)
+        nc.vector.tensor_copy(dst[:, :64], src[:, :64])
+        nc.vector.tensor_copy(dst[:, 64:80], src[:, 64:80])
+        nc.scalar.copy(dst[:, 80:], src[:, 80:])
         for h in range(2):
             cols = slice(h * HALF, (h + 1) * HALF)
             nc.vector.quantize_mx(
@@ -187,7 +183,7 @@ def tile_picked_twcputbgap_none_p_kernel(
             )
 
         cand_words.append(
-            pick(word_table, cand_t[:, 16:], reuse.tile([P, HALF], U32, name="cand_words1", align_bytes=64, offset=8192 + 2048))
+            pick(word_table, cand_t[:, 16:], reuse.tile([P, HALF], U32, name="cand_words1", align_bytes=64, offset=8192))
         )
 
         def score(c, cols, bank):
@@ -205,20 +201,21 @@ def tile_picked_twcputbgap_none_p_kernel(
             )
             return acc
 
-        for c in range(C // P):
-            minus_s = keep.tile([P, S], F32, name="minus_s%d" % c)
-            if c == 0:
-                nc.scalar.activation(minus_s[:, :HALF], score(c, slice(0, HALF), 0)[:], COPY, scale=-0.0625)
-                nc.vector.tensor_scalar(minus_s[:, HALF:], score(c, slice(HALF, S), 1)[:], -0.0625, None, MULT)
-            elif c < 3:
-                nc.vector.tensor_scalar(minus_s[:], score(c, slice(0, S), 3 + c)[:], -0.0625, None, MULT)
-            else:
-                nc.scalar.activation(minus_s[:], score(c, slice(0, S), 3 + c)[:], COPY, scale=-0.0625)
-            edges = (0, 256, 512) if c < 3 else (0, 256, 384, 512)
+
+        def differences(c, edges):
             for lo, hi in zip(edges, edges[1:]):
                 lcols = slice(lo // 16, hi // 16)
                 first = keep.tile([P, hi - lo], F32, name="first%d_%d" % (c, lo))
-                nc.scalar.activation(first[:], minus_s[:].indirect(n3_t[:, lcols]), COPY)
+                nc.scalar.activation(first[:], minus_s[c][:].indirect(n3_t[:, lcols]), COPY, scale=-1.0)
                 result = keep.tile([P, hi - lo], F32, name="result%d_%d" % (c, lo))
-                nc.vector.tensor_tensor(result[:], minus_s[:].indirect(n4_t[:, lcols]), first[:], SUB)
+                nc.vector.tensor_tensor(result[:], minus_s[c][:].indirect(n4_t[:, lcols]), first[:], ADD)
                 nc.sync.dma_start(out[c * P : (c + 1) * P, lo:hi], result[:])
+
+        nc.scalar.activation(minus_s[0][:, :HALF], score(0, slice(0, HALF), 0)[:], COPY, scale=-0.0625)
+        nc.vector.tensor_scalar(minus_s[0][:, HALF:S], score(0, slice(HALF, S), 1)[:], -0.0625, None, MULT)
+        for c in (1, 2):
+            nc.vector.tensor_scalar(minus_s[c][:, :S], score(c, slice(0, S), 3 + c)[:], -0.0625, None, MULT)
+        for c in range(3):
+            differences(c, (0, S))
+        nc.scalar.activation(minus_s[3][:, :S], score(3, slice(0, S), 6)[:], COPY, scale=-0.0625)
+        differences(3, (0, 256, 384, 512))

@@ -83,8 +83,8 @@ def tile_picked_twcputbgap_none_p_kernel(
             return pick(word_table, lst[:], keep.tile([P, S], U32, name=name, align_bytes=64))
 
         def deal_weight(grouped, raw, h, on_scalar):
-            dst = grouped[:].rearrange("p (t m j) -> p m j t", t=PACK, j=PACK)[:, h * 64 : (h + 1) * 64]
-            src = raw[:].rearrange("p j (m t) -> p m j t", t=PACK)
+            dst = grouped[:].rearrange("p (t m j) -> p m t j", t=PACK, j=PACK)[:, h * 64 : (h + 1) * 64]
+            src = raw[:].rearrange("p j (m t) -> p m t j", t=PACK)
             if on_scalar:
                 nc.scalar.copy(dst, src)
             else:
@@ -218,4 +218,11 @@ def tile_picked_twcputbgap_none_p_kernel(
         for c in range(3):
             differences(c, (0, S))
         nc.scalar.activation(minus_s[3][:, :S], score(3, slice(0, S), 6)[:], COPY, scale=-0.0625)
-        differences(3, (0, 256, 384, 512))
+        differences(3, (0, HALF))
+        first = keep.tile([P, HALF], F32, name="last_first")
+        nc.scalar.activation(first[:], minus_s[3][:].indirect(n3_t[:, 16:]), COPY, scale=-1.0)
+        second = keep.tile([P, HALF], F32, name="last_second")
+        nc.scalar.activation(second[:], minus_s[3][:].indirect(n4_t[:, 16:]), COPY)
+        result = keep.tile([P, HALF], F32, name="last_result")
+        nc.vector.tensor_tensor(result[:], second[:], first[:], ADD)
+        nc.sync.dma_start(out[3 * P :, HALF:], result[:])

from contextlib import ExitStack

import concourse.mybir as mybir

K, T, S, H, W, C = 512, 2048, 512, 512, 256, 512
FLOPS = 2 * K * H * S * 2 + 2 * H * C * S

F32 = mybir.dt.float32
BF16 = mybir.dt.bfloat16
I32 = mybir.dt.int32
U32 = mybir.dt.uint32
U16 = mybir.dt.uint16
U8 = mybir.dt.uint8
FP8X4 = mybir.dt.float8_e4m3fn_x4
COPY = mybir.ActivationFunctionType.Copy
MULT = mybir.AluOpType.mult
SUB = mybir.AluOpType.subtract
ADD = mybir.AluOpType.add

P = 128
PACK = 4
HALF = 256


def tile_picked_twcputbgap_none_p_kernel(
    tc, x_words, x_scales, w1, w2, gs, offs, two, n1, n2, cand, n3, n4, out
):
    nc = tc.nc
    with ExitStack() as ctx:
        keep = ctx.enter_context(tc.tile_pool(name="keep", bufs=1))
        psum = ctx.enter_context(tc.psum_pool(name="psum", bufs=1))
        reuse = ctx.enter_context(tc.tile_pool(name="reuse", bufs=1))

        def load_list(src, name):
            tile = keep.tile(list(src.shape), U16, name=name)
            nc.sync.dma_start(tile[:], src)
            return tile

        def load_weight_half(w, h, name, raw=None):
            if raw is None:
                raw = keep.tile([P, PACK, HALF], F32, name=name)
            nc.sync.dma_start(raw[:], w.rearrange("(p j) c -> p j c", j=PACK)[:, :, h * HALF : (h + 1) * HALF])
            return raw

        scale_table = keep.tile([P, T], U8, name="scale_table")
        nc.gpsimd.memset(scale_table[:].bitcast(I32), 0)
        two_t = load_list(two, "two_t")
        w2_raw = [load_weight_half(w2, 0, "w2_raw0")]
        for q in range(4):
            nc.sync.dma_start(
                scale_table[32 * q : 32 * q + 4, :].bitcast(I32), x_scales[0, 4 * q : 4 * q + 4, :].bitcast(I32)
            )
        offs_t = load_list(offs, "offs_t")
        w2_raw.append(load_weight_half(w2, 1, "w2_raw1"))
        word_table = keep.tile([P, T], U32, name="word_table")
        nc.sync.dma_start(word_table[:].bitcast(I32), x_words[0].rearrange("p n t -> p (n t)").bitcast(I32))
        w1_raw = [load_weight_half(w1, 0, "w1_raw0", reuse.tile([P, PACK, HALF], F32, name="w1_raw0", offset=4096))]
        w1_raw.append(load_weight_half(w1, 1, "w1_raw1", reuse.tile([P, PACK, HALF], F32, name="w1_raw1", offset=0)))
        cand_t = load_list(cand, "cand_t")
        n2_t = load_list(n2, "n2_t")
        n1_t = load_list(n1, "n1_t")
        gs_t = keep.tile([P, PACK], F32, name="gs_t")
        nc.sync.dma_start(gs_t[:], gs.rearrange("(p t) o -> p (t o)", t=PACK))
        n3_t = load_list(n3, "n3_t")
        n4_t = load_list(n4, "n4_t")


        minus_half = keep.tile([P, W], F32, name="minus_half")
        nc.gpsimd.memset(minus_half[:], -0.5)

        minus_s = [keep.tile([P, S + 16], F32, name="minus_s%d" % c) for c in range(C // P)]
        for tile in minus_s:
            nc.gpsimd.memset(tile[:, S:], 0.0)

        def pick(table, lst, picked):
            nc.vector.tensor_copy(picked[:], table[:].indirect(lst))
            return picked

        def pick_scales(lst, name):
            return pick(scale_table, lst[:], keep.tile([P, S], U8, name=name, align_bytes=64))

        def pick_words(lst, name):
            return pick(word_table, lst[:], keep.tile([P, S], U32, name=name, align_bytes=64))

        def deal_weight(grouped, raw, h, on_scalar):
            dst = grouped[:].rearrange("p (t m j) -> p m t j", t=PACK, j=PACK)[:, h * 64 : (h + 1) * 64]
            src = raw[:].rearrange("p j (m t) -> p m t j", t=PACK)
            if on_scalar:
                nc.scalar.copy(dst, src)
            else:
                nc.vector.tensor_copy(dst, src)

        def quantise(grouped, name):
            codes = keep.tile([P, 512], U32, name=name + "_codes", align_bytes=64)
            scales = keep.tile([P, 512], U8, name=name + "_scales", align_bytes=64)
            nc.vector.quantize_mx(out=codes[:].bitcast(FP8X4), scales=scales[:], in_=grouped)
            return codes, scales

        def product(lhs, lhs_scales, t, rhs, rhs_scales, bank):
            acc = psum.tile([P, 512], F32, name="acc", tag="bank%d" % bank)
            cols = slice(t * P, (t + 1) * P)
            nc.tensor.matmul_mx(
                out=acc[:],
                lhsT=lhs[:, cols].bitcast(FP8X4),
                lhsT_scale=lhs_scales[:, cols],
                rhs=rhs[:].bitcast(FP8X4),
                rhs_scale=rhs_scales[:],
                start=True,
                stop=True,
            )
            return acc

        two_scales = pick_scales(two_t, "two_scales")
        offs_scales = pick_scales(offs_t, "offs_scales")
        w2_grouped = keep.tile([P, PACK * H], BF16, name="w2_grouped", align_bytes=64)
        w1_grouped = keep.tile([P, PACK * H], BF16, name="w1_grouped", align_bytes=64)
        deal_weight(w2_grouped, w2_raw[0], 0, True)
        deal_weight(w2_grouped, w2_raw[1], 1, True)
        w2_codes, w2_scales = quantise(w2_grouped[:], "w2")
        two_words = pick_words(two_t, "two_words")
        offs_words = pick_words(offs_t, "offs_words")
        deal_weight(w1_grouped, w1_raw[0], 0, True)
        deal_weight(w1_grouped, w1_raw[1], 1, False)
        w1_codes, w1_scales = quantise(w1_grouped[:], "w1")
        cand_words = [pick(word_table, cand_t[:, :16], reuse.tile([P, HALF], U32, name="cand_words0", align_bytes=64, offset=0))]
        cand_scales = pick(scale_table, cand_t[:], reuse.tile([P, C], U8, name="cand_scales", align_bytes=64, offset=4 * C))

        d_acc = [product(w2_codes, w2_scales, t, two_words, two_scales, t) for t in range(2)]
        y_acc = [product(w1_codes, w1_scales, t, offs_words, offs_scales, 2 + t) for t in range(PACK)]


        def empty_d(t):
            if t < 3:
                d_rows = reuse.tile([P, S], F32, name="d_rows%d" % t, offset=4096 + 2048 * t)
            else:
                d_rows = keep.tile([P, S], F32, name="d_rows%d" % t)
            nc.scalar.copy(d_rows[:], d_acc[t][:])
            return d_rows

        def fetch(rows, lst, factor, name):
            picked = keep.tile([P, W], F32, name=name)
            nc.scalar.activation(picked[:], rows[:].indirect(lst[:]), COPY, scale=factor)
            return picked

        ds = [keep.tile([P, S], F32, name="ds%d" % t) for t in range(PACK)]
        d_rows = [empty_d(t) for t in range(2)]
        d_twice = [fetch(d_rows[t], n2_t, 2.0, "d_twice%d" % t) for t in range(2)]
        for t in range(2):
            nc.scalar.copy(ds[t][:], y_acc[t][:])
            d_acc.append(product(w2_codes, w2_scales, 2 + t, two_words, two_scales, 2 + t))
        gaps = []
        for t in range(2):
            gap = keep.tile([P, W], F32, name="gap%d" % t)
            nc.vector.tensor_tensor(gap[:], ds[t][:].indirect(n1_t[:]), d_twice[t][:], SUB)
            gaps.append(gap)
        nc.vector.tensor_tensor(ds[0][:].indirect(n1_t[:]), gaps[0][:], minus_half[:], MULT)
        for t in range(2, PACK):
            nc.scalar.copy(ds[t][:], y_acc[t][:])
            rows = empty_d(t)
            y_picked = fetch(ds[t], n1_t, -0.5, "y_picked%d" % t)
            d_picked = fetch(rows, n2_t, 1.0, "d_picked%d" % t)
            nc.vector.tensor_tensor(ds[t][:].indirect(n1_t[:]), d_picked[:], y_picked[:], ADD)
        nc.scalar.activation(ds[1][:].indirect(n1_t[:]), gaps[1][:], COPY, scale=-0.5)
        z_planes = reuse.tile([P, PACK, S], BF16, name="z_planes", offset=8192)
        for t in (0, 2, 3):
            nc.vector.tensor_scalar(z_planes[:, t, :], ds[t][:], gs_t[:, t : t + 1], None, MULT)
        nc.scalar.activation(z_planes[:, 1, :], ds[1][:], COPY, scale=gs_t[:, 1:2])

        z_grouped = keep.tile([P, PACK * S], BF16, name="z_grouped", align_bytes=64)
        z_codes = keep.tile([P, S], U32, name="z_codes", align_bytes=64)
        z_scales = keep.tile([P, S], U8, name="z_scales", align_bytes=64)
        dst = z_grouped[:].rearrange("p (c i t) -> p c t i", i=4, t=PACK)
        src = z_planes[:].rearrange("p t (c i) -> p c t i", i=4)
        nc.vector.tensor_copy(dst[:, :64], src[:, :64])
        nc.vector.tensor_copy(dst[:, 64:80], src[:, 64:80])
        nc.scalar.copy(dst[:, 80:], src[:, 80:])
        for h in range(2):
            cols = slice(h * HALF, (h + 1) * HALF)
            nc.vector.quantize_mx(
                out=z_codes[:, cols].bitcast(FP8X4),
                scales=z_scales[:, cols],
                in_=z_grouped[:, PACK * h * HALF : PACK * (h + 1) * HALF],
            )

        cand_words.append(
            pick(word_table, cand_t[:, 16:], reuse.tile([P, HALF], U32, name="cand_words1", align_bytes=64, offset=8192))
        )

        def score(c, cols, bank):
            width = cols.stop - cols.start
            acc = psum.tile([P, width], F32, name="acc", tag="bank%d" % bank)
            rows = slice(c * P, (c + 1) * P)
            nc.tensor.matmul_mx(
                out=acc[:],
                lhsT=cand_words[c // 2][:, (c % 2) * P : (c % 2 + 1) * P].bitcast(FP8X4),
                lhsT_scale=cand_scales[:, rows],
                rhs=z_codes[:, cols].bitcast(FP8X4),
                rhs_scale=z_scales[:, cols],
                start=True,
                stop=True,
            )
            return acc


        def differences(c, edges):
            for lo, hi in zip(edges, edges[1:]):
                lcols = slice(lo // 16, hi // 16)
                first = keep.tile([P, hi - lo], F32, name="first%d_%d" % (c, lo))
                nc.scalar.activation(first[:], minus_s[c][:].indirect(n3_t[:, lcols]), COPY, scale=-1.0)
                result = keep.tile([P, hi - lo], F32, name="result%d_%d" % (c, lo))
                nc.vector.tensor_tensor(result[:], minus_s[c][:].indirect(n4_t[:, lcols]), first[:], ADD)
                nc.sync.dma_start(out[c * P : (c + 1) * P, lo:hi], result[:])

        nc.scalar.activation(minus_s[0][:, :HALF], score(0, slice(0, HALF), 0)[:], COPY, scale=-0.0625)
        nc.vector.tensor_scalar(minus_s[0][:, HALF:S], score(0, slice(HALF, S), 1)[:], -0.0625, None, MULT)
        for c in (1, 2):
            nc.vector.tensor_scalar(minus_s[c][:, :S], score(c, slice(0, S), 3 + c)[:], -0.0625, None, MULT)
        for c in range(3):
            differences(c, (0, S))
        nc.scalar.activation(minus_s[3][:, :S], score(3, slice(0, S), 6)[:], COPY, scale=-0.0625)
        differences(3, (0, HALF))
        first = keep.tile([P, HALF], F32, name="last_first")
        nc.scalar.activation(first[:], minus_s[3][:].indirect(n3_t[:, 16:]), COPY, scale=-1.0)
        second = keep.tile([P, HALF], F32, name="last_second")
        nc.scalar.activation(second[:], minus_s[3][:].indirect(n4_t[:, 16:]), COPY)
        result = keep.tile([P, HALF], F32, name="last_result")
        nc.vector.tensor_tensor(result[:], second[:], first[:], ADD)
        nc.sync.dma_start(out[3 * P :, HALF:], result[:])
